import numpy as np
import ml_dtypes


def mxq(x, axis, fmt="e4m3"):
    dtype, down = {"e4m3": (ml_dtypes.float8_e4m3fn, 7), "e5m2": (ml_dtypes.float8_e5m2, 14)}[fmt]
    v = np.moveaxis(np.asarray(x, np.float32).astype(ml_dtypes.bfloat16).astype(np.float64), axis, -1)
    blocks = v.reshape(v.shape[:-1] + (-1, 32))
    amax = np.abs(blocks).max(-1, keepdims=True)
    byte = np.maximum(np.where(amax > 0, np.frexp(amax)[1] - 1 + 127, 0) - down, 1)
    scale = np.exp2(byte - 127.0)
    codes = (blocks / scale).astype(np.float32).astype(dtype).astype(np.float64)
    return np.moveaxis((codes * scale).reshape(v.shape), -1, axis)


WIDE = False


def mx_kscale(k):
    if not WIDE:
        return np.ones(k)
    levels = np.array([10, -10, 5, -5, 0])
    if k % 512:
        return np.exp2(np.random.permutation(np.resize(levels, k // 32))).repeat(32)
    a = np.empty((k // 512, 16))
    for p in range(k // 512):
        a[p, :8] = np.random.permutation(np.resize(levels, 8))
        for g in range(8):
            far = levels[np.abs(levels - a[p, g]) >= 10]
            a[p, g + 8] = far[np.random.randint(len(far))]
    return np.exp2(a.ravel()).repeat(32)


def f64(x):
    return np.asarray(x).astype(np.float64)


def striped(idx):
    return np.tile(np.asarray(idx).reshape(-1, 16).T, (8, 1)).astype(np.uint16)


def unstriped(offs):
    return offs[:16].T.reshape(-1).astype(np.int64)


E2M1 = np.array([0.0, 0.5, 1.0, 1.5, 2.0, 3.0, 4.0, 6.0, -0.0, -0.5, -1.0, -1.5, -2.0, -3.0, -4.0, -6.0])


def pack_weight(w, fmt):
    k, n = w.shape
    w = f64(np.asarray(w, np.float32).astype(ml_dtypes.bfloat16)).reshape(k // 32, 32, n)
    amax = np.abs(w).max(1)
    if fmt == "e4m3":
        byte = np.frexp(amax)[1] - 1 + 127 - 7
    else:
        mant, ex = np.frexp(amax / 6.0)
        byte = np.where(mant > 0.5, ex, ex - 1) + 127
    byte = np.clip(np.where(amax > 0, byte, 1), 1, 254)
    scaled = (w * np.exp2(127.0 - byte)[:, None, :]).reshape(k, n).astype(np.float32)
    by_word = np.ascontiguousarray(scaled.reshape(k // 512, 128, 4, n).transpose(0, 1, 3, 2))
    if fmt == "e4m3":
        words = by_word.astype(ml_dtypes.float8_e4m3fn).view(np.uint8)
    else:
        c = by_word.astype(ml_dtypes.float4_e2m1fn).view(np.uint8) & 0xF
        words = (c[..., 0::2] | (c[..., 1::2] << 4)).reshape(k // 512, 128, 2 * n)
    return np.ascontiguousarray(words), np.ascontiguousarray(byte.astype(np.uint8).reshape(k // 512, 16, n))


def unpack_weight(words, scales, fmt):
    g, _, n = scales.shape
    words = np.ascontiguousarray(words).reshape(g, 128, n, -1)
    if fmt == "e4m3":
        vals = words.view(ml_dtypes.float8_e4m3fn).astype(np.float64)
    else:
        nib = np.empty((g, 128, n, 4), np.uint8)
        nib[..., 0::2] = words & 0xF
        nib[..., 1::2] = words >> 4
        vals = E2M1[nib]
    vals = vals * np.repeat(np.exp2(scales.astype(np.float64) - 127.0), 8, axis=1)[..., None]
    return vals.transpose(0, 1, 3, 2).reshape(g * 512, n)


B, N, T, D, NQ = 1, 1024, 4096, 512, 128
SEG = 16


def setup_inputs():
    n = np.random.standard_normal
    pages = np.random.permutation(T // 16)[:B * N // 16]
    idx = (pages[:, None] * 16 + np.arange(16)[None, :]).reshape(-1)
    s = mx_kscale(D)[:, None]
    kp = pack_weight(n((D, T)) / s, "e4m3")
    return {
        "qT": (n((B, D, NQ)) * s * (1.00 / np.sqrt(D))).astype(np.float32),
        "k_words": kp[0],
        "k_scales": kp[1],
        "offs": striped(idx),
    }


def reference(qT, k_words, k_scales, offs):
    idx = unstriped(offs)
    pick = lambda x, which: x[:, which].reshape(x.shape[0], B, -1).transpose(1, 0, 2)
    k = unpack_weight(k_words, k_scales, "e4m3")
    kg = pick(k, idx)
    qq = mxq(f64(qT), 1, "e4m3")
    a = qq.transpose(0, 2, 1) @ kg
    mu = a.reshape(B, NQ, N // SEG, SEG).mean(-1)
    y = np.square(a).reshape(B, NQ, N // SEG, SEG).mean(-1) - np.square(mu)
    return y

@@ -1,0 +1,91 @@
+from contextlib import ExitStack
+
+import concourse.mybir as mybir
+
+F32 = mybir.dt.float32
+BF16 = mybir.dt.bfloat16
+I32 = mybir.dt.int32
+U32 = mybir.dt.uint32
+U16 = mybir.dt.uint16
+U8 = mybir.dt.uint8
+FP8X4 = mybir.dt.float8_e4m3fn_x4
+ALU = mybir.AluOpType
+
+P = 128
+PACK = 4
+T = 4096
+N = 1024
+NQ = 128
+PAGE = 16
+PAGES = N // PAGE
+GATHER = 512
+BANK = 256
+FLOPS = 2 * 512 * NQ * N
+
+
+def tile_attend_page_var_kernel(tc, qT, k_words, k_scales, offs, out):
+    nc = tc.nc
+    with ExitStack() as ctx:
+        held = ctx.enter_context(tc.tile_pool(name="held", bufs=1))
+        psum = ctx.enter_context(tc.psum_pool(name="psum", bufs=1))
+
+        offsets = held.tile([P, N // 16], U16, name="offsets")
+        nc.sync.dma_start(offsets[:], offs)
+
+        q_raw = held.tile([P, PACK, NQ], F32, name="q_raw", align_bytes=64)
+        nc.sync.dma_start(q_raw[:], qT[0].rearrange("(p j) q -> p j q", j=PACK))
+
+        pool_words = held.tile([P, T], I32, name="pool_words", align_bytes=64)
+        nc.sync.dma_start(pool_words[:], k_words[0].rearrange("p t r -> p (t r)").bitcast(I32))
+
+        pool_scales = held.tile([P, T // 4], I32, name="pool_scales", tag="shared0", align_bytes=64)
+        nc.vector.memset(pool_scales[:], 0)
+        nc.scalar.dma_start(pool_scales[4:P:8, :], k_scales[0].bitcast(I32))
+        key_scales = held.tile([P, N // 4], I32, name="key_scales", align_bytes=64)
+        nc.vector.memset(key_scales[:], 0)
+
+        q_bf = held.tile([P, NQ, PACK], BF16, name="q_bf", align_bytes=64)
+        nc.vector.tensor_scalar(q_bf[:], q_raw[:].rearrange("p j q -> p q j"), 0.25, None, ALU.mult)
+
+        scale_rows = held.tile([P, N], U8, name="scale_rows", align_bytes=64)
+        nc.vector.tensor_copy(scale_rows[:], pool_scales[:].bitcast(U8).indirect(offsets[:]))
+        for quad in range(4):
+            nc.scalar.dma_start(
+                key_scales[32 * quad : 32 * quad + 4, :],
+                scale_rows[32 * quad + 4 : 32 * quad + 32 : 8, :].bitcast(I32),
+            )
+
+        q_codes = held.tile([P, NQ], U32, name="q_codes", align_bytes=64)
+        q_scales = held.tile([P, NQ], U8, name="q_scales", align_bytes=64)
+        nc.vector.quantize_mx(
+            out=q_codes[:].bitcast(FP8X4), scales=q_scales[:], in_=q_bf[:].rearrange("p q j -> p (q j)")
+        )
+
+        key_words = []
+        for g in range(N // GATHER):
+            words = held.tile([P, GATHER], U32, name="key_words%d" % g, tag="shared%d" % g, align_bytes=64)
+            cols = slice(g * GATHER // 16, (g + 1) * GATHER // 16)
+            nc.vector.tensor_copy(words[:], pool_words[:].bitcast(U32).indirect(offsets[:, cols]))
+            key_words.append(words)
+
+        stats = held.tile([P, 3, PAGES], F32, name="stats", align_bytes=64)
+        for g in range(N // GATHER):
+            for h in range(GATHER // BANK):
+                first = g * GATHER + h * BANK
+                scores = psum.tile([P, BANK], F32, name="scores%d" % (first // BANK))
+                nc.tensor.matmul_mx(
+                    out=scores[:],
+                    lhsT=q_codes[:].bitcast(FP8X4),
+                    lhsT_scale=q_scales[:],
+                    rhs=key_words[g][:, h * BANK : (h + 1) * BANK].bitcast(FP8X4),
+                    rhs_scale=key_scales[:].bitcast(U8)[:, first : first + BANK],
+                    start=True,
+                    stop=True,
+                )
+                for pair in range(BANK // (2 * PAGE)):
+                    page = first // PAGE + 2 * pair
+                    nc.vector.bn_stats(
+                        stats[:, :, page : page + 2].rearrange("p k e -> p e k"),
+                        scores[:, 2 * PAGE * pair : 2 * PAGE * (pair + 1)].rearrange("p (e r) -> p r e", e=2),
+                    )
+        nc.sync.dma_start(out[0], stats[:, 2, :])

@@ -38,9 +38,9 @@ def tile_attend_page_var_kernel(tc, qT, k_words, k_scales, offs, out):
         pool_words = held.tile([P, T], I32, name="pool_words", align_bytes=64)
         nc.sync.dma_start(pool_words[:], k_words[0].rearrange("p t r -> p (t r)").bitcast(I32))
 
-        pool_scales = held.tile([P, T // 4], I32, name="pool_scales", tag="shared0", align_bytes=64)
-        nc.vector.memset(pool_scales[:], 0)
-        nc.scalar.dma_start(pool_scales[4:P:8, :], k_scales[0].bitcast(I32))
+        pool_scales = held.tile([P, T // 4], I32, name="pool_scales", tag="shared1", align_bytes=64)
+        nc.scalar.dma_start(pool_scales[P - 16 : P, :], k_scales[0].bitcast(I32))
+        nc.vector.memset(pool_scales[0 : P - 16, :], 0)
         key_scales = held.tile([P, N // 4], I32, name="key_scales", align_bytes=64)
         nc.vector.memset(key_scales[:], 0)
 
@@ -52,7 +52,7 @@ def tile_attend_page_var_kernel(tc, qT, k_words, k_scales, offs, out):
         for quad in range(4):
             nc.scalar.dma_start(
                 key_scales[32 * quad : 32 * quad + 4, :],
-                scale_rows[32 * quad + 4 : 32 * quad + 32 : 8, :].bitcast(I32),
+                scale_rows[P - 16 + 4 * quad : P - 12 + 4 * quad, :].bitcast(I32),
             )
 
         q_codes = held.tile([P, NQ], U32, name="q_codes", align_bytes=64)
@@ -61,16 +61,19 @@ def tile_attend_page_var_kernel(tc, qT, k_words, k_scales, offs, out):
             out=q_codes[:].bitcast(FP8X4), scales=q_scales[:], in_=q_bf[:].rearrange("p q j -> p (q j)")
         )
 
-        key_words = []
-        for g in range(N // GATHER):
+        key_words = {}
+        for g in reversed(range(N // GATHER)):
             words = held.tile([P, GATHER], U32, name="key_words%d" % g, tag="shared%d" % g, align_bytes=64)
             cols = slice(g * GATHER // 16, (g + 1) * GATHER // 16)
             nc.vector.tensor_copy(words[:], pool_words[:].bitcast(U32).indirect(offsets[:, cols]))
-            key_words.append(words)
+            key_words[g] = words
 
-        stats = held.tile([P, 3, PAGES], F32, name="stats", align_bytes=64)
-        for g in range(N // GATHER):
-            for h in range(GATHER // BANK):
+        side = BANK // PAGE
+        stats = held.tile([P, 2 * side + PAGES], F32, name="stats", align_bytes=64)
+        variance = stats[:, 2 * side :]
+        spread = stats[:, 0 : 3 * side].rearrange("p (k j) -> p j k", k=3)
+        for g in reversed(range(N // GATHER)):
+            for h in reversed(range(GATHER // BANK)):
                 first = g * GATHER + h * BANK
                 scores = psum.tile([P, BANK], F32, name="scores%d" % (first // BANK))
                 nc.tensor.matmul_mx(
@@ -82,10 +85,18 @@ def tile_attend_page_var_kernel(tc, qT, k_words, k_scales, offs, out):
                     start=True,
                     stop=True,
                 )
-                for pair in range(BANK // (2 * PAGE)):
+                last = first == 0
+                pairs = BANK // (2 * PAGE)
+                dense = None if last else held.tile([P, pairs, 6], F32, name="dense%d" % (first // BANK), align_bytes=64)
+                for pair in range(pairs):
                     page = first // PAGE + 2 * pair
                     nc.vector.bn_stats(
-                        stats[:, :, page : page + 2].rearrange("p k e -> p e k"),
+                        spread[:, page : page + 2, :] if last else dense[:, pair, :],
                         scores[:, 2 * PAGE * pair : 2 * PAGE * (pair + 1)].rearrange("p (e r) -> p r e", e=2),
                     )
-        nc.sync.dma_start(out[0], stats[:, 2, :])
+                if not last:
+                    nc.scalar.copy(
+                        variance[:, first // PAGE : (first + BANK) // PAGE],
+                        dense[:].rearrange("p a (e k) -> p (a e) k", k=3)[:, :, 2],
+                    )
+        nc.sync.dma_start(out[0], variance)

@@ -10,6 +10,7 @@ U16 = mybir.dt.uint16
 U8 = mybir.dt.uint8
 FP8X4 = mybir.dt.float8_e4m3fn_x4
 ALU = mybir.AluOpType
+ACT = mybir.ActivationFunctionType
 
 P = 128
 PACK = 4
@@ -68,35 +69,55 @@ def tile_attend_page_var_kernel(tc, qT, k_words, k_scales, offs, out):
             nc.vector.tensor_copy(words[:], pool_words[:].bitcast(U32).indirect(offsets[:, cols]))
             key_words[g] = words
 
-        side = BANK // PAGE
+        side = 16
         stats = held.tile([P, 2 * side + PAGES], F32, name="stats", align_bytes=64)
         variance = stats[:, 2 * side :]
         spread = stats[:, 0 : 3 * side].rearrange("p (k j) -> p j k", k=3)
-        for g in reversed(range(N // GATHER)):
-            for h in reversed(range(GATHER // BANK)):
-                first = g * GATHER + h * BANK
-                scores = psum.tile([P, BANK], F32, name="scores%d" % (first // BANK))
-                nc.tensor.matmul_mx(
-                    out=scores[:],
-                    lhsT=q_codes[:].bitcast(FP8X4),
-                    lhsT_scale=q_scales[:],
-                    rhs=key_words[g][:, h * BANK : (h + 1) * BANK].bitcast(FP8X4),
-                    rhs_scale=key_scales[:].bitcast(U8)[:, first : first + BANK],
-                    start=True,
-                    stop=True,
+        dense = held.tile([P, (PAGES - side - 8) // 2, 6], F32, name="dense", align_bytes=64)
+        shrunk = held.tile([P, 8, PAGE], F32, name="shrunk", align_bytes=64)
+        squares = held.tile([P, 8, PAGE], F32, name="squares", align_bytes=64)
+        neg_mean = held.tile([P, 8], F32, name="neg_mean", align_bytes=64)
+        for first, width in ((768, 128), (896, 128), (512, 256), (256, 256), (0, 256)):
+            scores = psum.tile([P, width], F32, name="scores%d" % first)
+            lo = first % GATHER
+            nc.tensor.matmul_mx(
+                out=scores[:],
+                lhsT=q_codes[:].bitcast(FP8X4),
+                lhsT_scale=q_scales[:],
+                rhs=key_words[first // GATHER][:, lo : lo + width].bitcast(FP8X4),
+                rhs_scale=key_scales[:].bitcast(U8)[:, first : first + width],
+                start=True,
+                stop=True,
+            )
+            if first == 896:
+                for j in range(8):
+                    nc.scalar.activation(
+                        shrunk[:, j, :],
+                        scores[:, PAGE * j : PAGE * (j + 1)],
+                        ACT.Copy,
+                        scale=-1.0 / PAGE,
+                        accum_out=neg_mean[:, j : j + 1],
+                    )
+                for j in range(8):
+                    page = first // PAGE + j
+                    nc.scalar.activation(
+                        squares[:, j, :],
+                        shrunk[:, j, :],
+                        ACT.Square,
+                        bias=neg_mean[:, j : j + 1],
+                        scale=-float(PAGE),
+                        accum_out=variance[:, page : page + 1],
+                    )
+                continue
+            for pair in range(width // (2 * PAGE)):
+                page = first // PAGE + 2 * pair
+                nc.vector.bn_stats(
+                    spread[:, page : page + 2, :] if page < side else dense[:, (page - side) // 2, :],
+                    scores[:, 2 * PAGE * pair : 2 * PAGE * (pair + 1)].rearrange("p (e r) -> p r e", e=2),
                 )
-                last = first == 0
-                pairs = BANK // (2 * PAGE)
-                dense = None if last else held.tile([P, pairs, 6], F32, name="dense%d" % (first // BANK), align_bytes=64)
-                for pair in range(pairs):
-                    page = first // PAGE + 2 * pair
-                    nc.vector.bn_stats(
-                        spread[:, page : page + 2, :] if last else dense[:, pair, :],
-                        scores[:, 2 * PAGE * pair : 2 * PAGE * (pair + 1)].rearrange("p (e r) -> p r e", e=2),
-                    )
-                if not last:
-                    nc.scalar.copy(
-                        variance[:, first // PAGE : (first + BANK) // PAGE],
-                        dense[:].rearrange("p a (e k) -> p (a e) k", k=3)[:, :, 2],
-                    )
+            if first == 256:
+                nc.scalar.copy(
+                    variance[:, side : PAGES - 8],
+                    dense[:].rearrange("p a (e k) -> p (a e) k", k=3)[:, :, 2],
+                )
         nc.sync.dma_start(out[0], variance)

@@ -77,7 +77,7 @@ def tile_attend_page_var_kernel(tc, qT, k_words, k_scales, offs, out):
         shrunk = held.tile([P, 8, PAGE], F32, name="shrunk", align_bytes=64)
         squares = held.tile([P, 8, PAGE], F32, name="squares", align_bytes=64)
         neg_mean = held.tile([P, 8], F32, name="neg_mean", align_bytes=64)
-        for first, width in ((768, 128), (896, 128), (512, 256), (256, 256), (0, 256)):
+        for first, width in ((768, 128), (896, 128), (640, 128), (512, 128), (384, 128), (256, 128), (128, 128), (0, 128)):
             scores = psum.tile([P, width], F32, name="scores%d" % first)
             lo = first % GATHER
             nc.tensor.matmul_mx(

@@ -45,9 +45,6 @@ def tile_attend_page_var_kernel(tc, qT, k_words, k_scales, offs, out):
         key_scales = held.tile([P, N // 4], I32, name="key_scales", align_bytes=64)
         nc.vector.memset(key_scales[:], 0)
 
-        q_bf = held.tile([P, NQ, PACK], BF16, name="q_bf", align_bytes=64)
-        nc.vector.tensor_scalar(q_bf[:], q_raw[:].rearrange("p j q -> p q j"), 0.25, None, ALU.mult)
-
         scale_rows = held.tile([P, N], U8, name="scale_rows", align_bytes=64)
         nc.vector.tensor_copy(scale_rows[:], pool_scales[:].bitcast(U8).indirect(offsets[:]))
         for quad in range(4):
@@ -55,6 +52,9 @@ def tile_attend_page_var_kernel(tc, qT, k_words, k_scales, offs, out):
                 key_scales[32 * quad : 32 * quad + 4, :],
                 scale_rows[P - 16 + 4 * quad : P - 12 + 4 * quad, :].bitcast(I32),
             )
+
+        q_bf = held.tile([P, NQ, PACK], BF16, name="q_bf", tag="shared1", align_bytes=64)
+        nc.vector.tensor_scalar(q_bf[:], q_raw[:].rearrange("p j q -> p q j"), 0.25, None, ALU.mult)
 
         q_codes = held.tile([P, NQ], U32, name="q_codes", align_bytes=64)
         q_scales = held.tile([P, NQ], U8, name="q_scales", align_bytes=64)
@@ -64,7 +64,7 @@ def tile_attend_page_var_kernel(tc, qT, k_words, k_scales, offs, out):
 
         key_words = {}
         for g in reversed(range(N // GATHER)):
-            words = held.tile([P, GATHER], U32, name="key_words%d" % g, tag="shared%d" % g, align_bytes=64)
+            words = held.tile([P, GATHER], U32, name="key_words%d" % g, align_bytes=64)
             cols = slice(g * GATHER // 16, (g + 1) * GATHER // 16)
             nc.vector.tensor_copy(words[:], pool_words[:].bitcast(U32).indirect(offsets[:, cols]))
             key_words[g] = words

@@ -19,9 +19,10 @@ N = 1024
 NQ = 128
 PAGE = 16
 PAGES = N // PAGE
-GATHER = 512
-BANK = 256
 FLOPS = 2 * 512 * NQ * N
+GATHER = 256
+SCALAR_PAGES = 12
+SIDE = 16
 
 
 def tile_attend_page_var_kernel(tc, qT, k_words, k_scales, offs, out):
@@ -69,15 +70,15 @@ def tile_attend_page_var_kernel(tc, qT, k_words, k_scales, offs, out):
             nc.vector.tensor_copy(words[:], pool_words[:].bitcast(U32).indirect(offsets[:, cols]))
             key_words[g] = words
 
-        side = 16
-        stats = held.tile([P, 2 * side + PAGES], F32, name="stats", align_bytes=64)
-        variance = stats[:, 2 * side :]
-        spread = stats[:, 0 : 3 * side].rearrange("p (k j) -> p j k", k=3)
-        dense = held.tile([P, (PAGES - side - 8) // 2, 6], F32, name="dense", align_bytes=64)
-        shrunk = held.tile([P, 8, PAGE], F32, name="shrunk", align_bytes=64)
-        squares = held.tile([P, 8, PAGE], F32, name="squares", align_bytes=64)
-        neg_mean = held.tile([P, 8], F32, name="neg_mean", align_bytes=64)
-        for first, width in ((768, 128), (896, 128), (640, 128), (512, 128), (384, 128), (256, 128), (128, 128), (0, 128)):
+        stats = held.tile([P, 2 * SIDE + PAGES], F32, name="stats", align_bytes=64)
+        variance = stats[:, 2 * SIDE :]
+        spread = stats[:, 0 : 3 * SIDE].rearrange("p (k j) -> p j k", k=3)
+        dense = held.tile([P, (PAGES - SIDE - SCALAR_PAGES) // 2, 6], F32, name="dense", align_bytes=64)
+        shrunk = held.tile([P, SCALAR_PAGES, PAGE], F32, name="shrunk", align_bytes=64)
+        squares = held.tile([P, SCALAR_PAGES, PAGE], F32, name="squares", align_bytes=64)
+        neg_mean = held.tile([P, SCALAR_PAGES], F32, name="neg_mean", align_bytes=64)
+        scalar_from = PAGES - SCALAR_PAGES
+        for first, width in ((896, 128), (832, 64), (768, 64), (512, 256), (256, 256), (128, 128), (0, 128)):
             scores = psum.tile([P, width], F32, name="scores%d" % first)
             lo = first % GATHER
             nc.tensor.matmul_mx(
@@ -89,35 +90,39 @@ def tile_attend_page_var_kernel(tc, qT, k_words, k_scales, offs, out):
                 start=True,
                 stop=True,
             )
-            if first == 896:
-                for j in range(8):
+            if first // PAGE >= scalar_from:
+                for j in range(width // PAGE):
+                    s = first // PAGE + j - scalar_from
                     nc.scalar.activation(
-                        shrunk[:, j, :],
+                        shrunk[:, s, :],
                         scores[:, PAGE * j : PAGE * (j + 1)],
                         ACT.Copy,
                         scale=-1.0 / PAGE,
-                        accum_out=neg_mean[:, j : j + 1],
-                    )
-                for j in range(8):
-                    page = first // PAGE + j
-                    nc.scalar.activation(
-                        squares[:, j, :],
-                        shrunk[:, j, :],
-                        ACT.Square,
-                        bias=neg_mean[:, j : j + 1],
-                        scale=-float(PAGE),
-                        accum_out=variance[:, page : page + 1],
+                        accum_out=neg_mean[:, s : s + 1],
                     )
                 continue
             for pair in range(width // (2 * PAGE)):
                 page = first // PAGE + 2 * pair
                 nc.vector.bn_stats(
-                    spread[:, page : page + 2, :] if page < side else dense[:, (page - side) // 2, :],
+                    spread[:, page : page + 2, :] if page < SIDE else dense[:, (page - SIDE) // 2, :],
                     scores[:, 2 * PAGE * pair : 2 * PAGE * (pair + 1)].rearrange("p (e r) -> p r e", e=2),
                 )
-            if first == 256:
-                nc.scalar.copy(
-                    variance[:, side : PAGES - 8],
+            if first == SIDE * PAGE:
+                nc.gpsimd.tensor_scalar(
+                    variance[:, SIDE:scalar_from],
                     dense[:].rearrange("p a (e k) -> p (a e) k", k=3)[:, :, 2],
+                    1.0,
+                    0.0,
+                    ALU.mult,
+                    ALU.add,
                 )
+        for s in reversed(range(SCALAR_PAGES)):
+            nc.scalar.activation(
+                squares[:, s, :],
+                shrunk[:, s, :],
+                ACT.Square,
+                bias=neg_mean[:, s : s + 1],
+                scale=-float(PAGE),
+                accum_out=variance[:, scalar_from + s : scalar_from + s + 1],
+            )
         nc.sync.dma_start(out[0], variance)

@@ -21,7 +21,8 @@ PAGE = 16
 PAGES = N // PAGE
 FLOPS = 2 * 512 * NQ * N
 GATHER = 256
-SCALAR_PAGES = 12
+SCALAR_PAGES = 10
+BANK = 128
 SIDE = 16
 
 
@@ -78,36 +79,49 @@ def tile_attend_page_var_kernel(tc, qT, k_words, k_scales, offs, out):
         squares = held.tile([P, SCALAR_PAGES, PAGE], F32, name="squares", align_bytes=64)
         neg_mean = held.tile([P, SCALAR_PAGES], F32, name="neg_mean", align_bytes=64)
         scalar_from = PAGES - SCALAR_PAGES
-        for first, width in ((896, 128), (832, 64), (768, 64), (512, 256), (256, 256), (128, 128), (0, 128)):
-            scores = psum.tile([P, width], F32, name="scores%d" % first)
+        bank_pages = BANK // PAGE
+        scores = {}
+        for bank in reversed(range(N // BANK)):
+            first = bank * BANK
+            scores[bank] = psum.tile([P, BANK], F32, name="scores%d" % bank)
             lo = first % GATHER
             nc.tensor.matmul_mx(
-                out=scores[:],
+                out=scores[bank][:],
                 lhsT=q_codes[:].bitcast(FP8X4),
                 lhsT_scale=q_scales[:],
-                rhs=key_words[first // GATHER][:, lo : lo + width].bitcast(FP8X4),
-                rhs_scale=key_scales[:].bitcast(U8)[:, first : first + width],
+                rhs=key_words[first // GATHER][:, lo : lo + BANK].bitcast(FP8X4),
+                rhs_scale=key_scales[:].bitcast(U8)[:, first : first + BANK],
                 start=True,
                 stop=True,
             )
-            if first // PAGE >= scalar_from:
-                for j in range(width // PAGE):
-                    s = first // PAGE + j - scalar_from
-                    nc.scalar.activation(
-                        shrunk[:, s, :],
-                        scores[:, PAGE * j : PAGE * (j + 1)],
-                        ACT.Copy,
-                        scale=-1.0 / PAGE,
-                        accum_out=neg_mean[:, s : s + 1],
-                    )
-                continue
-            for pair in range(width // (2 * PAGE)):
-                page = first // PAGE + 2 * pair
-                nc.vector.bn_stats(
-                    spread[:, page : page + 2, :] if page < SIDE else dense[:, (page - SIDE) // 2, :],
-                    scores[:, 2 * PAGE * pair : 2 * PAGE * (pair + 1)].rearrange("p (e r) -> p r e", e=2),
-                )
-            if first == SIDE * PAGE:
+
+        def page_scores(page, count):
+            lo = page % bank_pages * PAGE
+            return scores[page // bank_pages][:, lo : lo + count * PAGE]
+
+        def mean_pass(page):
+            s = page - scalar_from
+            nc.scalar.activation(
+                shrunk[:, s, :], page_scores(page, 1), ACT.Copy, scale=-1.0 / PAGE, accum_out=neg_mean[:, s : s + 1]
+            )
+
+        def square_pass(page):
+            s = page - scalar_from
+            nc.scalar.activation(
+                squares[:, s, :],
+                shrunk[:, s, :],
+                ACT.Square,
+                bias=neg_mean[:, s : s + 1],
+                scale=-float(PAGE),
+                accum_out=variance[:, page : page + 1],
+            )
+
+        for page in reversed(range(0, scalar_from, 2)):
+            nc.vector.bn_stats(
+                spread[:, page : page + 2, :] if page < SIDE else dense[:, (page - SIDE) // 2, :],
+                page_scores(page, 2).rearrange("p (e r) -> p r e", e=2),
+            )
+            if page == SIDE:
                 nc.gpsimd.tensor_scalar(
                     variance[:, SIDE:scalar_from],
                     dense[:].rearrange("p a (e k) -> p (a e) k", k=3)[:, :, 2],
@@ -116,13 +130,17 @@ def tile_attend_page_var_kernel(tc, qT, k_words, k_scales, offs, out):
                     ALU.mult,
                     ALU.add,
                 )
-        for s in reversed(range(SCALAR_PAGES)):
-            nc.scalar.activation(
-                squares[:, s, :],
-                shrunk[:, s, :],
-                ACT.Square,
-                bias=neg_mean[:, s : s + 1],
-                scale=-float(PAGE),
-                accum_out=variance[:, scalar_from + s : scalar_from + s + 1],
-            )
+
+        own = range(PAGES - bank_pages, PAGES)
+        shared = range(scalar_from, PAGES - bank_pages)
+        for page in own:
+            mean_pass(page)
+        for page in own[:2]:
+            square_pass(page)
+        for page in shared:
+            mean_pass(page)
+        for page in own[2:]:
+            square_pass(page)
+        for page in shared:
+            square_pass(page)
         nc.sync.dma_start(out[0], variance)

@@ -19,11 +19,9 @@ N = 1024
 NQ = 128
 PAGE = 16
 PAGES = N // PAGE
-FLOPS = 2 * 512 * NQ * N
 GATHER = 256
-SCALAR_PAGES = 10
-BANK = 128
-SIDE = 16
+BANK = 256
+FLOPS = 2 * 512 * NQ * N
 
 
 def tile_attend_page_var_kernel(tc, qT, k_words, k_scales, offs, out):
@@ -71,76 +69,55 @@ def tile_attend_page_var_kernel(tc, qT, k_words, k_scales, offs, out):
             nc.vector.tensor_copy(words[:], pool_words[:].bitcast(U32).indirect(offsets[:, cols]))
             key_words[g] = words
 
-        stats = held.tile([P, 2 * SIDE + PAGES], F32, name="stats", align_bytes=64)
-        variance = stats[:, 2 * SIDE :]
-        spread = stats[:, 0 : 3 * SIDE].rearrange("p (k j) -> p j k", k=3)
-        dense = held.tile([P, (PAGES - SIDE - SCALAR_PAGES) // 2, 6], F32, name="dense", align_bytes=64)
-        shrunk = held.tile([P, SCALAR_PAGES, PAGE], F32, name="shrunk", align_bytes=64)
-        squares = held.tile([P, SCALAR_PAGES, PAGE], F32, name="squares", align_bytes=64)
-        neg_mean = held.tile([P, SCALAR_PAGES], F32, name="neg_mean", align_bytes=64)
-        scalar_from = PAGES - SCALAR_PAGES
-        bank_pages = BANK // PAGE
-        scores = {}
-        for bank in reversed(range(N // BANK)):
-            first = bank * BANK
-            scores[bank] = psum.tile([P, BANK], F32, name="scores%d" % bank)
+        side = 16
+        stats = held.tile([P, 2 * side + PAGES], F32, name="stats", align_bytes=64)
+        variance = stats[:, 2 * side :]
+        spread = stats[:, 0 : 3 * side].rearrange("p (k j) -> p j k", k=3)
+        dense = held.tile([P, (PAGES - side - 8) // 2, 6], F32, name="dense", align_bytes=64)
+        shrunk = held.tile([P, 8, PAGE], F32, name="shrunk", align_bytes=64)
+        squares = held.tile([P, 8, PAGE], F32, name="squares", align_bytes=64)
+        neg_mean = held.tile([P, 8], F32, name="neg_mean", align_bytes=64)
+        for first, width in ((896, 128), (768, 128), (640, 128), (512, 128), (384, 128), (256, 128), (128, 128), (0, 128)):
+            scores = psum.tile([P, width], F32, name="scores%d" % first)
             lo = first % GATHER
             nc.tensor.matmul_mx(
-                out=scores[bank][:],
+                out=scores[:],
                 lhsT=q_codes[:].bitcast(FP8X4),
                 lhsT_scale=q_scales[:],
-                rhs=key_words[first // GATHER][:, lo : lo + BANK].bitcast(FP8X4),
-                rhs_scale=key_scales[:].bitcast(U8)[:, first : first + BANK],
+                rhs=key_words[first // GATHER][:, lo : lo + width].bitcast(FP8X4),
+                rhs_scale=key_scales[:].bitcast(U8)[:, first : first + width],
                 start=True,
                 stop=True,
             )
-
-        def page_scores(page, count):
-            lo = page % bank_pages * PAGE
-            return scores[page // bank_pages][:, lo : lo + count * PAGE]
-
-        def mean_pass(page):
-            s = page - scalar_from
-            nc.scalar.activation(
-                shrunk[:, s, :], page_scores(page, 1), ACT.Copy, scale=-1.0 / PAGE, accum_out=neg_mean[:, s : s + 1]
-            )
-
-        def square_pass(page):
-            s = page - scalar_from
-            nc.scalar.activation(
-                squares[:, s, :],
-                shrunk[:, s, :],
-                ACT.Square,
-                bias=neg_mean[:, s : s + 1],
-                scale=-float(PAGE),
-                accum_out=variance[:, page : page + 1],
-            )
-
-        for page in reversed(range(0, scalar_from, 2)):
-            nc.vector.bn_stats(
-                spread[:, page : page + 2, :] if page < SIDE else dense[:, (page - SIDE) // 2, :],
-                page_scores(page, 2).rearrange("p (e r) -> p r e", e=2),
-            )
-            if page == SIDE:
-                nc.gpsimd.tensor_scalar(
-                    variance[:, SIDE:scalar_from],
-                    dense[:].rearrange("p a (e k) -> p (a e) k", k=3)[:, :, 2],
-                    1.0,
-                    0.0,
-                    ALU.mult,
-                    ALU.add,
+            if first == 896:
+                for j in range(8):
+                    nc.scalar.activation(
+                        shrunk[:, j, :],
+                        scores[:, PAGE * j : PAGE * (j + 1)],
+                        ACT.Copy,
+                        scale=-1.0 / PAGE,
+                        accum_out=neg_mean[:, j : j + 1],
+                    )
+                for j in range(8):
+                    page = first // PAGE + j
+                    nc.scalar.activation(
+                        squares[:, j, :],
+                        shrunk[:, j, :],
+                        ACT.Square,
+                        bias=neg_mean[:, j : j + 1],
+                        scale=-float(PAGE),
+                        accum_out=variance[:, page : page + 1],
+                    )
+                continue
+            for pair in range(width // (2 * PAGE)):
+                page = first // PAGE + 2 * pair
+                nc.vector.bn_stats(
+                    spread[:, page : page + 2, :] if page < side else dense[:, (page - side) // 2, :],
+                    scores[:, 2 * PAGE * pair : 2 * PAGE * (pair + 1)].rearrange("p (e r) -> p r e", e=2),
                 )
-
-        own = range(PAGES - bank_pages, PAGES)
-        shared = range(scalar_from, PAGES - bank_pages)
-        for page in own:
-            mean_pass(page)
-        for page in own[:2]:
-            square_pass(page)
-        for page in shared:
-            mean_pass(page)
-        for page in own[2:]:
-            square_pass(page)
-        for page in shared:
-            square_pass(page)
+            if first == 256:
+                nc.scalar.copy(
+                    variance[:, side : PAGES - 8],
+                    dense[:].rearrange("p a (e k) -> p (a e) k", k=3)[:, :, 2],
+                )
         nc.sync.dma_start(out[0], variance)

@@ -19,8 +19,7 @@ N = 1024
 NQ = 128
 PAGE = 16
 PAGES = N // PAGE
-GATHER = 256
-BANK = 256
+CHUNKS = ((768, 256), (512, 256), (256, 256), (0, 256))
 FLOPS = 2 * 512 * NQ * N
 
 
@@ -63,28 +62,32 @@ def tile_attend_page_var_kernel(tc, qT, k_words, k_scales, offs, out):
         )
 
         key_words = {}
-        for g in reversed(range(N // GATHER)):
-            words = held.tile([P, GATHER], U32, name="key_words%d" % g, align_bytes=64)
-            cols = slice(g * GATHER // 16, (g + 1) * GATHER // 16)
+        for start, count in CHUNKS:
+            words = held.tile([P, count], U32, name="key_words%d" % start, align_bytes=64)
+            cols = slice(start // 16, (start + count) // 16)
             nc.vector.tensor_copy(words[:], pool_words[:].bitcast(U32).indirect(offsets[:, cols]))
-            key_words[g] = words
+            for lo in range(0, count, 128):
+                key_words[start + lo] = words[:, lo : lo + 128]
 
-        side = 16
-        stats = held.tile([P, 2 * side + PAGES], F32, name="stats", align_bytes=64)
-        variance = stats[:, 2 * side :]
-        spread = stats[:, 0 : 3 * side].rearrange("p (k j) -> p j k", k=3)
-        dense = held.tile([P, (PAGES - side - 8) // 2, 6], F32, name="dense", align_bytes=64)
+        side = 24
+        packs = (PAGES - side - 8) // 2
+        lead = 2
+        base = lead + 6 * packs - 2
+        stats = held.tile([P, base + 2 * side + PAGES], F32, name="stats", align_bytes=64)
+        variance = stats[:, base + 2 * side :]
+        spread = stats[:, base : base + 3 * side].rearrange("p (k j) -> p j k", k=3)
+        dense = stats[:, lead : lead + 6 * packs].rearrange("p (a s) -> p a s", s=6)
+        packed = dense.rearrange("p a (e k) -> p (a e) k", k=3)[:, :, 2]
         shrunk = held.tile([P, 8, PAGE], F32, name="shrunk", align_bytes=64)
         squares = held.tile([P, 8, PAGE], F32, name="squares", align_bytes=64)
         neg_mean = held.tile([P, 8], F32, name="neg_mean", align_bytes=64)
         for first, width in ((896, 128), (768, 128), (640, 128), (512, 128), (384, 128), (256, 128), (128, 128), (0, 128)):
             scores = psum.tile([P, width], F32, name="scores%d" % first)
-            lo = first % GATHER
             nc.tensor.matmul_mx(
                 out=scores[:],
                 lhsT=q_codes[:].bitcast(FP8X4),
                 lhsT_scale=q_scales[:],
-                rhs=key_words[first // GATHER][:, lo : lo + width].bitcast(FP8X4),
+                rhs=key_words[first].bitcast(FP8X4),
                 rhs_scale=key_scales[:].bitcast(U8)[:, first : first + width],
                 start=True,
                 stop=True,
@@ -109,15 +112,14 @@ def tile_attend_page_var_kernel(tc, qT, k_words, k_scales, offs, out):
                         accum_out=variance[:, page : page + 1],
                     )
                 continue
-            for pair in range(width // (2 * PAGE)):
+            for pair in reversed(range(width // (2 * PAGE))) if first == 0 else range(width // (2 * PAGE)):
                 page = first // PAGE + 2 * pair
                 nc.vector.bn_stats(
-                    spread[:, page : page + 2, :] if page < side else dense[:, (page - side) // 2, :],
+                    spread[:, page : page + 2, :] if page < side else dense[:, (page - side - 8) // 2 % packs, :],
                     scores[:, 2 * PAGE * pair : 2 * PAGE * (pair + 1)].rearrange("p (e r) -> p r e", e=2),
                 )
-            if first == 256:
-                nc.scalar.copy(
-                    variance[:, side : PAGES - 8],
-                    dense[:].rearrange("p a (e k) -> p (a e) k", k=3)[:, :, 2],
-                )
+            if first == 512:
+                nc.scalar.copy(variance[:, side + 8 : PAGES - 8], packed[:, : 2 * packs - 8])
+            if first == 384:
+                nc.scalar.copy(variance[:, side : side + 8], packed[:, 2 * packs - 8 :])
         nc.sync.dma_start(out[0], variance)

@@ -29,22 +29,22 @@ def tile_attend_page_var_kernel(tc, qT, k_words, k_scales, offs, out):
         held = ctx.enter_context(tc.tile_pool(name="held", bufs=1))
         psum = ctx.enter_context(tc.psum_pool(name="psum", bufs=1))
 
-        offsets = held.tile([P, N // 16], U16, name="offsets")
+        offsets = held.tile([P, N // 16], U16, name="offsets", align_bytes=256)
         nc.sync.dma_start(offsets[:], offs)
 
-        q_raw = held.tile([P, PACK, NQ], F32, name="q_raw", align_bytes=64)
+        q_raw = held.tile([P, PACK, NQ], F32, name="q_raw", align_bytes=256)
         nc.sync.dma_start(q_raw[:], qT[0].rearrange("(p j) q -> p j q", j=PACK))
 
-        pool_words = held.tile([P, T], I32, name="pool_words", align_bytes=64)
+        pool_words = held.tile([P, T], I32, name="pool_words", align_bytes=256)
         nc.sync.dma_start(pool_words[:], k_words[0].rearrange("p t r -> p (t r)").bitcast(I32))
 
-        pool_scales = held.tile([P, T // 4], I32, name="pool_scales", tag="shared1", align_bytes=64)
+        pool_scales = held.tile([P, T // 4], I32, name="pool_scales", tag="shared1", align_bytes=256)
         nc.scalar.dma_start(pool_scales[P - 16 : P, :], k_scales[0].bitcast(I32))
         nc.vector.memset(pool_scales[0 : P - 16, :], 0)
-        key_scales = held.tile([P, N // 4], I32, name="key_scales", align_bytes=64)
+        key_scales = held.tile([P, N // 4], I32, name="key_scales", align_bytes=256)
         nc.vector.memset(key_scales[:], 0)
 
-        scale_rows = held.tile([P, N], U8, name="scale_rows", align_bytes=64)
+        scale_rows = held.tile([P, N], U8, name="scale_rows", align_bytes=256)
         nc.vector.tensor_copy(scale_rows[:], pool_scales[:].bitcast(U8).indirect(offsets[:]))
         for quad in range(4):
             nc.scalar.dma_start(
@@ -52,65 +52,65 @@ def tile_attend_page_var_kernel(tc, qT, k_words, k_scales, offs, out):
                 scale_rows[P - 16 + 4 * quad : P - 12 + 4 * quad, :].bitcast(I32),
             )
 
-        q_bf = held.tile([P, NQ, PACK], BF16, name="q_bf", tag="shared1", align_bytes=64)
+        q_bf = held.tile([P, NQ, PACK], BF16, name="q_bf", tag="shared1", align_bytes=256)
         nc.vector.tensor_scalar(q_bf[:], q_raw[:].rearrange("p j q -> p q j"), 0.25, None, ALU.mult)
 
-        q_codes = held.tile([P, NQ], U32, name="q_codes", align_bytes=64)
-        q_scales = held.tile([P, NQ], U8, name="q_scales", align_bytes=64)
+        q_codes = held.tile([P, NQ], U32, name="q_codes", align_bytes=256)
+        q_scales = held.tile([P, NQ], U8, name="q_scales", align_bytes=256)
         nc.vector.quantize_mx(
             out=q_codes[:].bitcast(FP8X4), scales=q_scales[:], in_=q_bf[:].rearrange("p q j -> p (q j)")
         )
 
         key_words = {}
         for start, count in CHUNKS:
-            words = held.tile([P, count], U32, name="key_words%d" % start, align_bytes=64)
+            words = held.tile([P, count], U32, name="key_words%d" % start, align_bytes=256)
             cols = slice(start // 16, (start + count) // 16)
             nc.vector.tensor_copy(words[:], pool_words[:].bitcast(U32).indirect(offsets[:, cols]))
-            for lo in range(0, count, 128):
-                key_words[start + lo] = words[:, lo : lo + 128]
+            key_words[start] = words
 
         side = 24
         packs = (PAGES - side - 8) // 2
-        lead = 2
+        lead = 50
         base = lead + 6 * packs - 2
-        stats = held.tile([P, base + 2 * side + PAGES], F32, name="stats", align_bytes=64)
+        stats = held.tile([P, base + 2 * side + PAGES], F32, name="stats", align_bytes=256)
         variance = stats[:, base + 2 * side :]
         spread = stats[:, base : base + 3 * side].rearrange("p (k j) -> p j k", k=3)
         dense = stats[:, lead : lead + 6 * packs].rearrange("p (a s) -> p a s", s=6)
         packed = dense.rearrange("p a (e k) -> p (a e) k", k=3)[:, :, 2]
-        shrunk = held.tile([P, 8, PAGE], F32, name="shrunk", align_bytes=64)
-        squares = held.tile([P, 8, PAGE], F32, name="squares", align_bytes=64)
-        neg_mean = held.tile([P, 8], F32, name="neg_mean", align_bytes=64)
-        for first, width in ((896, 128), (768, 128), (640, 128), (512, 128), (384, 128), (256, 128), (128, 128), (0, 128)):
-            scores = psum.tile([P, width], F32, name="scores%d" % first)
+        shrunk = held.tile([P, 8, PAGE], F32, name="shrunk", align_bytes=256)
+        squares = held.tile([P, 8, PAGE], F32, name="squares", align_bytes=256)
+        neg_mean = held.tile([P, 8], F32, name="neg_mean", align_bytes=256)
+        for first, width in ((960, 64), (768, 128), (896, 64), (640, 128), (512, 128), (384, 128), (256, 128), (128, 128), (0, 128)):
+            scores = psum.tile([P, width], F32, name="scores%d" % first, tag="bank%d" % (first or 960))
             nc.tensor.matmul_mx(
                 out=scores[:],
                 lhsT=q_codes[:].bitcast(FP8X4),
                 lhsT_scale=q_scales[:],
-                rhs=key_words[first].bitcast(FP8X4),
+                rhs=key_words[first // 256 * 256][:, first % 256 : first % 256 + width].bitcast(FP8X4),
                 rhs_scale=key_scales[:].bitcast(U8)[:, first : first + width],
                 start=True,
                 stop=True,
             )
-            if first == 896:
-                for j in range(8):
+            if first >= 896:
+                for j in range(4):
+                    s = (first - 896) // PAGE + j
                     nc.scalar.activation(
-                        shrunk[:, j, :],
+                        shrunk[:, s, :],
                         scores[:, PAGE * j : PAGE * (j + 1)],
                         ACT.Copy,
                         scale=-1.0 / PAGE,
-                        accum_out=neg_mean[:, j : j + 1],
+                        accum_out=neg_mean[:, s : s + 1],
                     )
-                for j in range(8):
-                    page = first // PAGE + j
-                    nc.scalar.activation(
-                        squares[:, j, :],
-                        shrunk[:, j, :],
-                        ACT.Square,
-                        bias=neg_mean[:, j : j + 1],
-                        scale=-float(PAGE),
-                        accum_out=variance[:, page : page + 1],
-                    )
+                if first == 896:
+                    for s in (4, 5, 6, 7, 0, 1, 2, 3):
+                        nc.scalar.activation(
+                            squares[:, s, :],
+                            shrunk[:, s, :],
+                            ACT.Square,
+                            bias=neg_mean[:, s : s + 1],
+                            scale=-float(PAGE),
+                            accum_out=variance[:, 56 + s : 57 + s],
+                        )
                 continue
             for pair in reversed(range(width // (2 * PAGE))) if first == 0 else range(width // (2 * PAGE)):
                 page = first // PAGE + 2 * pair

@@ -46,10 +46,14 @@ def tile_attend_page_var_kernel(tc, qT, k_words, k_scales, offs, out):
 
         scale_rows = held.tile([P, N], U8, name="scale_rows", align_bytes=256)
         nc.vector.tensor_copy(scale_rows[:], pool_scales[:].bitcast(U8).indirect(offsets[:]))
-        for quad in range(4):
-            nc.scalar.dma_start(
-                key_scales[32 * quad : 32 * quad + 4, :],
-                scale_rows[P - 16 + 4 * quad : P - 12 + 4 * quad, :].bitcast(I32),
+        for quad, lo, hi in (
+            [(quad, 256, N) for quad in range(4)]
+            + [(quad, 0, 256) for quad in (0, 1)]
+            + [(quad, lo, lo + 128) for lo in (128, 0) for quad in (2, 3)]
+        ):
+            nc.sync.dma_start(
+                key_scales[32 * quad : 32 * quad + 4, lo // 4 : hi // 4],
+                scale_rows[P - 16 + 4 * quad : P - 12 + 4 * quad, lo:hi].bitcast(I32),
             )
 
         q_bf = held.tile([P, NQ, PACK], BF16, name="q_bf", tag="shared1", align_bytes=256)

@@ -32,15 +32,16 @@ def tile_attend_page_var_kernel(tc, qT, k_words, k_scales, offs, out):
         offsets = held.tile([P, N // 16], U16, name="offsets", align_bytes=256)
         nc.sync.dma_start(offsets[:], offs)
 
+        pool_scales = held.tile([P, T // 4], I32, name="pool_scales", tag="shared1", align_bytes=256)
+        nc.scalar.dma_start(pool_scales[P - 16 : P, :], k_scales[0].bitcast(I32))
+        nc.vector.memset(pool_scales[0 : P - 16, :], 0)
+
         q_raw = held.tile([P, PACK, NQ], F32, name="q_raw", align_bytes=256)
         nc.sync.dma_start(q_raw[:], qT[0].rearrange("(p j) q -> p j q", j=PACK))
 
         pool_words = held.tile([P, T], I32, name="pool_words", align_bytes=256)
         nc.sync.dma_start(pool_words[:], k_words[0].rearrange("p t r -> p (t r)").bitcast(I32))
 
-        pool_scales = held.tile([P, T // 4], I32, name="pool_scales", tag="shared1", align_bytes=256)
-        nc.scalar.dma_start(pool_scales[P - 16 : P, :], k_scales[0].bitcast(I32))
-        nc.vector.memset(pool_scales[0 : P - 16, :], 0)
         key_scales = held.tile([P, N // 4], I32, name="key_scales", align_bytes=256)
         nc.vector.memset(key_scales[:], 0)
 
@@ -51,7 +52,7 @@ def tile_attend_page_var_kernel(tc, qT, k_words, k_scales, offs, out):
             + [(quad, 0, 256) for quad in (0, 1)]
             + [(quad, lo, lo + 128) for lo in (128, 0) for quad in (2, 3)]
         ):
-            nc.sync.dma_start(
+            (nc.scalar if lo == 256 else nc.sync).dma_start(
                 key_scales[32 * quad : 32 * quad + 4, lo // 4 : hi // 4],
                 scale_rows[P - 16 + 4 * quad : P - 12 + 4 * quad, lo:hi].bitcast(I32),
             )

@@ -85,46 +85,48 @@ def tile_attend_page_var_kernel(tc, qT, k_words, k_scales, offs, out):
         shrunk = held.tile([P, 8, PAGE], F32, name="shrunk", align_bytes=256)
         squares = held.tile([P, 8, PAGE], F32, name="squares", align_bytes=256)
         neg_mean = held.tile([P, 8], F32, name="neg_mean", align_bytes=256)
-        for first, width in ((960, 64), (768, 128), (896, 64), (640, 128), (512, 128), (384, 128), (256, 128), (128, 128), (0, 128)):
-            scores = psum.tile([P, width], F32, name="scores%d" % first, tag="bank%d" % (first or 960))
-            nc.tensor.matmul_mx(
-                out=scores[:],
-                lhsT=q_codes[:].bitcast(FP8X4),
-                lhsT_scale=q_scales[:],
-                rhs=key_words[first // 256 * 256][:, first % 256 : first % 256 + width].bitcast(FP8X4),
-                rhs_scale=key_scales[:].bitcast(U8)[:, first : first + width],
-                start=True,
-                stop=True,
-            )
-            if first >= 896:
-                for j in range(4):
-                    s = (first - 896) // PAGE + j
+        for group in ((896,), (768, 640), (512, 384, 256), (128, 0)):
+            low = min(group)
+            scores = psum.tile([P, 128 * len(group)], F32, name="scores%d" % low)
+            for first in group:
+                nc.tensor.matmul_mx(
+                    out=scores[:, first - low : first - low + 128],
+                    lhsT=q_codes[:].bitcast(FP8X4),
+                    lhsT_scale=q_scales[:],
+                    rhs=key_words[first // 256 * 256][:, first % 256 : first % 256 + 128].bitcast(FP8X4),
+                    rhs_scale=key_scales[:].bitcast(U8)[:, first : first + 128],
+                    start=True,
+                    stop=True,
+                )
+            if low == 896:
+                for s in range(8):
                     nc.scalar.activation(
                         shrunk[:, s, :],
-                        scores[:, PAGE * j : PAGE * (j + 1)],
+                        scores[:, PAGE * s : PAGE * (s + 1)],
                         ACT.Copy,
                         scale=-1.0 / PAGE,
                         accum_out=neg_mean[:, s : s + 1],
                     )
-                if first == 896:
-                    for s in (4, 5, 6, 7, 0, 1, 2, 3):
-                        nc.scalar.activation(
-                            squares[:, s, :],
-                            shrunk[:, s, :],
-                            ACT.Square,
-                            bias=neg_mean[:, s : s + 1],
-                            scale=-float(PAGE),
-                            accum_out=variance[:, 56 + s : 57 + s],
-                        )
+                for s in (3, 2, 1, 0, 7, 6, 5, 4):
+                    nc.scalar.activation(
+                        squares[:, s, :],
+                        shrunk[:, s, :],
+                        ACT.Square,
+                        bias=neg_mean[:, s : s + 1],
+                        scale=-float(PAGE),
+                        accum_out=variance[:, 56 + s : 57 + s],
+                    )
                 continue
-            for pair in reversed(range(width // (2 * PAGE))) if first == 0 else range(width // (2 * PAGE)):
-                page = first // PAGE + 2 * pair
-                nc.vector.bn_stats(
-                    spread[:, page : page + 2, :] if page < side else dense[:, (page - side - 8) // 2 % packs, :],
-                    scores[:, 2 * PAGE * pair : 2 * PAGE * (pair + 1)].rearrange("p (e r) -> p r e", e=2),
-                )
-            if first == 512:
-                nc.scalar.copy(variance[:, side + 8 : PAGES - 8], packed[:, : 2 * packs - 8])
-            if first == 384:
-                nc.scalar.copy(variance[:, side : side + 8], packed[:, 2 * packs - 8 :])
+            for first in group:
+                for pair in reversed(range(4)) if first == 0 else range(4):
+                    page = first // PAGE + 2 * pair
+                    col = PAGE * page - low
+                    nc.vector.bn_stats(
+                        spread[:, page : page + 2, :] if page < side else dense[:, (page - side - 8) // 2 % packs, :],
+                        scores[:, col : col + 2 * PAGE].rearrange("p (e r) -> p r e", e=2),
+                    )
+                if first == 512:
+                    nc.scalar.copy(variance[:, side + 8 : PAGES - 8], packed[:, : 2 * packs - 8])
+                if first == 384:
+                    nc.scalar.copy(variance[:, side : side + 8], packed[:, 2 * packs - 8 :])
         nc.sync.dma_start(out[0], variance)

@@ -74,7 +74,9 @@ def tile_attend_page_var_kernel(tc, qT, k_words, k_scales, offs, out):
             key_words[start] = words
 
         side = 24
-        packs = (PAGES - side - 8) // 2
+        late = 8
+        own = 8
+        packs = (PAGES - side - own) // 2
         lead = 50
         base = lead + 6 * packs - 2
         stats = held.tile([P, base + 2 * side + PAGES], F32, name="stats", align_bytes=256)
@@ -82,51 +84,58 @@ def tile_attend_page_var_kernel(tc, qT, k_words, k_scales, offs, out):
         spread = stats[:, base : base + 3 * side].rearrange("p (k j) -> p j k", k=3)
         dense = stats[:, lead : lead + 6 * packs].rearrange("p (a s) -> p a s", s=6)
         packed = dense.rearrange("p a (e k) -> p (a e) k", k=3)[:, :, 2]
-        shrunk = held.tile([P, 8, PAGE], F32, name="shrunk", align_bytes=256)
-        squares = held.tile([P, 8, PAGE], F32, name="squares", align_bytes=256)
-        neg_mean = held.tile([P, 8], F32, name="neg_mean", align_bytes=256)
-        for group in ((896,), (768, 640), (512, 384, 256), (128, 0)):
-            low = min(group)
-            scores = psum.tile([P, 128 * len(group)], F32, name="scores%d" % low)
-            for first in group:
+        shrunk = held.tile([P, own, PAGE], F32, name="shrunk", align_bytes=256)
+        squares = held.tile([P, own, PAGE], F32, name="squares", align_bytes=256)
+        neg_mean = held.tile([P, own], F32, name="neg_mean", align_bytes=256)
+        mine = PAGES - own
+        done = []
+        for group in (((896, 128),), ((768, 128),), ((640, 128),), ((512, 128),), ((384, 128),), ((256, 128),), ((128, 128),), ((0, 128),),):
+            low = min(first for first, width in group)
+            scores = psum.tile([P, sum(width for first, width in group)], F32, name="scores%d" % low, tag="bank%d" % low)
+            for first, width in group:
+                start = max(s for s, count in CHUNKS if s <= first)
                 nc.tensor.matmul_mx(
-                    out=scores[:, first - low : first - low + 128],
+                    out=scores[:, first - low : first - low + width],
                     lhsT=q_codes[:].bitcast(FP8X4),
                     lhsT_scale=q_scales[:],
-                    rhs=key_words[first // 256 * 256][:, first % 256 : first % 256 + 128].bitcast(FP8X4),
-                    rhs_scale=key_scales[:].bitcast(U8)[:, first : first + 128],
+                    rhs=key_words[start][:, first - start : first - start + width].bitcast(FP8X4),
+                    rhs_scale=key_scales[:].bitcast(U8)[:, first : first + width],
                     start=True,
                     stop=True,
                 )
-            if low == 896:
-                for s in range(8):
-                    nc.scalar.activation(
-                        shrunk[:, s, :],
-                        scores[:, PAGE * s : PAGE * (s + 1)],
-                        ACT.Copy,
-                        scale=-1.0 / PAGE,
-                        accum_out=neg_mean[:, s : s + 1],
-                    )
-                for s in (3, 2, 1, 0, 7, 6, 5, 4):
-                    nc.scalar.activation(
-                        squares[:, s, :],
-                        shrunk[:, s, :],
-                        ACT.Square,
-                        bias=neg_mean[:, s : s + 1],
-                        scale=-float(PAGE),
-                        accum_out=variance[:, 56 + s : 57 + s],
-                    )
-                continue
-            for first in group:
-                for pair in reversed(range(4)) if first == 0 else range(4):
-                    page = first // PAGE + 2 * pair
+            for first, width in group:
+                pages = range(first // PAGE, (first + width) // PAGE)
+                pairs = [page for page in pages if page < mine and page % 2 == 0]
+                for page in reversed(pairs) if first == 0 else pairs:
                     col = PAGE * page - low
                     nc.vector.bn_stats(
-                        spread[:, page : page + 2, :] if page < side else dense[:, (page - side - 8) // 2 % packs, :],
+                        spread[:, page : page + 2, :] if page < side else dense[:, (page - side - late) // 2 % packs, :],
                         scores[:, col : col + 2 * PAGE].rearrange("p (e r) -> p r e", e=2),
                     )
+                for page in pages:
+                    if page >= mine:
+                        s = page - mine
+                        nc.scalar.activation(
+                            shrunk[:, s, :],
+                            scores[:, PAGE * page - low : PAGE * (page + 1) - low],
+                            ACT.Copy,
+                            scale=-1.0 / PAGE,
+                            accum_out=neg_mean[:, s : s + 1],
+                        )
+                        done.append(s)
+                if len(done) == own:
+                    for s in done:
+                        nc.scalar.activation(
+                            squares[:, s, :],
+                            shrunk[:, s, :],
+                            ACT.Square,
+                            bias=neg_mean[:, s : s + 1],
+                            scale=-float(PAGE),
+                            accum_out=variance[:, mine + s : mine + s + 1],
+                        )
+                    done.clear()
                 if first == 512:
-                    nc.scalar.copy(variance[:, side + 8 : PAGES - 8], packed[:, : 2 * packs - 8])
+                    nc.scalar.copy(variance[:, side + late : mine], packed[:, : 2 * packs - late])
                 if first == 384:
-                    nc.scalar.copy(variance[:, side : side + 8], packed[:, 2 * packs - 8 :])
+                    nc.scalar.copy(variance[:, side : side + late], packed[:, 2 * packs - late :])
         nc.sync.dma_start(out[0], variance)

@@ -124,7 +124,7 @@ def tile_attend_page_var_kernel(tc, qT, k_words, k_scales, offs, out):
                         )
                         done.append(s)
                 if len(done) == own:
-                    for s in done:
+                    for s in (3, 2, 1, 0, 7, 6, 5, 4):
                         nc.scalar.activation(
                             squares[:, s, :],
                             shrunk[:, s, :],

from contextlib import ExitStack

import concourse.mybir as mybir

F32 = mybir.dt.float32
BF16 = mybir.dt.bfloat16
I32 = mybir.dt.int32
U32 = mybir.dt.uint32
U16 = mybir.dt.uint16
U8 = mybir.dt.uint8
FP8X4 = mybir.dt.float8_e4m3fn_x4
ALU = mybir.AluOpType
ACT = mybir.ActivationFunctionType

P = 128
PACK = 4
T = 4096
N = 1024
NQ = 128
PAGE = 16
PAGES = N // PAGE
CHUNKS = ((768, 256), (512, 256), (256, 256), (0, 256))
FLOPS = 2 * 512 * NQ * N


def tile_attend_page_var_kernel(tc, qT, k_words, k_scales, offs, out):
    nc = tc.nc
    with ExitStack() as ctx:
        held = ctx.enter_context(tc.tile_pool(name="held", bufs=1))
        psum = ctx.enter_context(tc.psum_pool(name="psum", bufs=1))

        offsets = held.tile([P, N // 16], U16, name="offsets", align_bytes=256)
        nc.sync.dma_start(offsets[:], offs)

        pool_scales = held.tile([P, T // 4], I32, name="pool_scales", tag="shared1", align_bytes=256)
        nc.scalar.dma_start(pool_scales[P - 16 : P, :], k_scales[0].bitcast(I32))
        nc.vector.memset(pool_scales[0 : P - 16, :], 0)

        q_raw = held.tile([P, PACK, NQ], F32, name="q_raw", align_bytes=256)
        nc.sync.dma_start(q_raw[:], qT[0].rearrange("(p j) q -> p j q", j=PACK))

        pool_words = held.tile([P, T], I32, name="pool_words", align_bytes=256)
        nc.sync.dma_start(pool_words[:], k_words[0].rearrange("p t r -> p (t r)").bitcast(I32))

        key_scales = held.tile([P, N // 4], I32, name="key_scales", align_bytes=256)
        nc.vector.memset(key_scales[:], 0)

        scale_rows = held.tile([P, N], U8, name="scale_rows", align_bytes=256)
        nc.vector.tensor_copy(scale_rows[:], pool_scales[:].bitcast(U8).indirect(offsets[:]))
        for quad, lo, hi in (
            [(quad, 256, N) for quad in range(4)]
            + [(quad, 0, 256) for quad in (0, 1)]
            + [(quad, lo, lo + 128) for lo in (128, 0) for quad in (2, 3)]
        ):
            (nc.scalar if lo == 256 else nc.sync).dma_start(
                key_scales[32 * quad : 32 * quad + 4, lo // 4 : hi // 4],
                scale_rows[P - 16 + 4 * quad : P - 12 + 4 * quad, lo:hi].bitcast(I32),
            )

        q_bf = held.tile([P, NQ, PACK], BF16, name="q_bf", tag="shared1", align_bytes=256)
        nc.vector.tensor_scalar(q_bf[:], q_raw[:].rearrange("p j q -> p q j"), 0.25, None, ALU.mult)

        q_codes = held.tile([P, NQ], U32, name="q_codes", align_bytes=256)
        q_scales = held.tile([P, NQ], U8, name="q_scales", align_bytes=256)
        nc.vector.quantize_mx(
            out=q_codes[:].bitcast(FP8X4), scales=q_scales[:], in_=q_bf[:].rearrange("p q j -> p (q j)")
        )

        key_words = {}
        for start, count in CHUNKS:
            words = held.tile([P, count], U32, name="key_words%d" % start, align_bytes=256)
            cols = slice(start // 16, (start + count) // 16)
            nc.vector.tensor_copy(words[:], pool_words[:].bitcast(U32).indirect(offsets[:, cols]))
            key_words[start] = words

        side = 24
        late = 8
        own = 8
        packs = (PAGES - side - own) // 2
        lead = 50
        base = lead + 6 * packs - 2
        stats = held.tile([P, base + 2 * side + PAGES], F32, name="stats", align_bytes=256)
        variance = stats[:, base + 2 * side :]
        spread = stats[:, base : base + 3 * side].rearrange("p (k j) -> p j k", k=3)
        dense = stats[:, lead : lead + 6 * packs].rearrange("p (a s) -> p a s", s=6)
        packed = dense.rearrange("p a (e k) -> p (a e) k", k=3)[:, :, 2]
        shrunk = held.tile([P, own, PAGE], F32, name="shrunk", align_bytes=256)
        squares = held.tile([P, own, PAGE], F32, name="squares", align_bytes=256)
        neg_mean = held.tile([P, own], F32, name="neg_mean", align_bytes=256)
        mine = PAGES - own
        done = []
        for group in (((896, 128),), ((768, 128),), ((640, 128),), ((512, 128),), ((384, 128),), ((256, 128),), ((128, 128),), ((0, 128),),):
            low = min(first for first, width in group)
            scores = psum.tile([P, sum(width for first, width in group)], F32, name="scores%d" % low, tag="bank%d" % low)
            for first, width in group:
                start = max(s for s, count in CHUNKS if s <= first)
                nc.tensor.matmul_mx(
                    out=scores[:, first - low : first - low + width],
                    lhsT=q_codes[:].bitcast(FP8X4),
                    lhsT_scale=q_scales[:],
                    rhs=key_words[start][:, first - start : first - start + width].bitcast(FP8X4),
                    rhs_scale=key_scales[:].bitcast(U8)[:, first : first + width],
                    start=True,
                    stop=True,
                )
            for first, width in group:
                pages = range(first // PAGE, (first + width) // PAGE)
                pairs = [page for page in pages if page < mine and page % 2 == 0]
                for page in reversed(pairs) if first == 0 else pairs:
                    col = PAGE * page - low
                    nc.vector.bn_stats(
                        spread[:, page : page + 2, :] if page < side else dense[:, (page - side - late) // 2 % packs, :],
                        scores[:, col : col + 2 * PAGE].rearrange("p (e r) -> p r e", e=2),
                    )
                for page in pages:
                    if page >= mine:
                        s = page - mine
                        nc.scalar.activation(
                            shrunk[:, s, :],
                            scores[:, PAGE * page - low : PAGE * (page + 1) - low],
                            ACT.Copy,
                            scale=-1.0 / PAGE,
                            accum_out=neg_mean[:, s : s + 1],
                        )
                        done.append(s)
                if len(done) == own:
                    for s in (3, 2, 1, 0, 7, 6, 5, 4):
                        nc.scalar.activation(
                            squares[:, s, :],
                            shrunk[:, s, :],
                            ACT.Square,
                            bias=neg_mean[:, s : s + 1],
                            scale=-float(PAGE),
                            accum_out=variance[:, mine + s : mine + s + 1],
                        )
                    done.clear()
                if first == 512:
                    nc.scalar.copy(variance[:, side + late : mine], packed[:, : 2 * packs - late])
                if first == 384:
                    nc.scalar.copy(variance[:, side : side + late], packed[:, 2 * packs - late :])
        nc.sync.dma_start(out[0], variance)
